import numpy as np
import ml_dtypes


def mxq(x, axis, fmt="e4m3"):
    dtype, down = {"e4m3": (ml_dtypes.float8_e4m3fn, 7), "e5m2": (ml_dtypes.float8_e5m2, 14)}[fmt]
    v = np.moveaxis(np.asarray(x, np.float32).astype(ml_dtypes.bfloat16).astype(np.float64), axis, -1)
    blocks = v.reshape(v.shape[:-1] + (-1, 32))
    amax = np.abs(blocks).max(-1, keepdims=True)
    byte = np.maximum(np.where(amax > 0, np.frexp(amax)[1] - 1 + 127, 0) - down, 1)
    scale = np.exp2(byte - 127.0)
    codes = (blocks / scale).astype(np.float32).astype(dtype).astype(np.float64)
    return np.moveaxis((codes * scale).reshape(v.shape), -1, axis)


WIDE = False


def mx_kscale(k):
    if not WIDE:
        return np.ones(k)
    levels = np.array([10, -10, 5, -5, 0])
    if k % 512:
        return np.exp2(np.random.permutation(np.resize(levels, k // 32))).repeat(32)
    a = np.empty((k // 512, 16))
    for p in range(k // 512):
        a[p, :8] = np.random.permutation(np.resize(levels, 8))
        for g in range(8):
            far = levels[np.abs(levels - a[p, g]) >= 10]
            a[p, g + 8] = far[np.random.randint(len(far))]
    return np.exp2(a.ravel()).repeat(32)


def f64(x):
    return np.asarray(x).astype(np.float64)


def striped(idx):
    return np.tile(idx.reshape(-1, 16).T, (8, 1)).astype(np.uint16)


def unstriped(offs):
    return offs[:16].T.reshape(-1).astype(np.int64)


def striped8(idx):
    return np.concatenate([x.reshape(-1, 16).T for x in idx]).astype(np.uint16)


def runs(offs, k):
    lists = np.stack([offs[16 * r : 16 * r + 16].T.reshape(-1) for r in range(8)]).astype(np.int64)
    return lists[np.arange(k) % 512 // 64]


def pack_weight(w):
    k, n = w.shape
    w = f64(np.asarray(w, np.float32).astype(ml_dtypes.bfloat16)).reshape(k // 32, 32, n)
    amax = np.abs(w).max(1)
    byte = np.clip(np.where(amax > 0, np.frexp(amax)[1] - 1 + 127 - 7, 1), 1, 254)
    scaled = (w * np.exp2(127.0 - byte)[:, None, :]).reshape(k, n).astype(np.float32)
    words = np.ascontiguousarray(scaled.reshape(k // 512, 128, 4, n).transpose(0, 1, 3, 2)).astype(ml_dtypes.float8_e4m3fn).view(np.uint8)
    return words, np.ascontiguousarray(byte.astype(np.uint8).reshape(k // 512, 16, n))


def unpack_weight(words, scales):
    g, p, n, _ = words.shape
    vals = np.ascontiguousarray(words).view(ml_dtypes.float8_e4m3fn).astype(np.float64) * np.repeat(np.exp2(scales.astype(np.float64) - 127.0), 8, axis=1)[..., None]
    return vals.transpose(0, 1, 3, 2).reshape(g * 512, n)

def planes(y):
    n, m = y.shape
    v = y.astype(np.float32).astype(ml_dtypes.bfloat16).astype(np.float64).reshape(n // 32, 32, m)
    top = np.abs(v).max(1)
    byte = np.clip(np.where(top > 0, np.frexp(top)[1] - 1 + 127 - 7, 1), 1, 254)
    codes = (v * np.exp2(127.0 - byte)[:, None, :]).reshape(n, m).astype(np.float32).astype(ml_dtypes.float8_e4m3fn).view(np.uint8)
    words = codes.reshape(n // 512, 128, 4, m).transpose(0, 1, 3, 2)
    return np.ascontiguousarray(words), np.ascontiguousarray(byte.astype(np.uint8).reshape(n // 512, 16, m))


K, T, S, V, H = 512, 2048, 512, 512, 512


def setup_inputs():
    n = np.random.standard_normal
    s = mx_kscale(K)[:, None]
    u = mx_kscale(S)
    packed_xT = pack_weight(n((K, T)) * s)
    packed_w1 = pack_weight(n((K, H)) / np.sqrt(K) / s)
    packed_w2 = pack_weight(n((K, H)) / np.sqrt(K) / s)
    packed_w3 = pack_weight(n((K, H)) / np.sqrt(K) / s)
    return {
        "x_words": packed_xT[0],
        "x_scales": packed_xT[1],
        "w1_words": packed_w1[0],
        "w1_scales": packed_w1[1],
        "w2_words": packed_w2[0],
        "w2_scales": packed_w2[1],
        "w3_words": packed_w3[0],
        "w3_scales": packed_w3[1],
        "ga": (np.random.uniform(0.5, 1.5, (H, 1)) * u[:, None]).astype(np.float32),
        "gb": (np.random.uniform(0.5, 1.5, (H, 1)) / u[:, None]).astype(np.float32),
        "offs": striped(np.random.permutation(T)[:S]),
        "two": striped(np.random.permutation(T)[:S]),
        "n1": striped8(np.stack([np.random.permutation(S) for _ in range(8)])),
        "n2": striped8(np.stack([np.random.permutation(S) for _ in range(8)])),
        "three": striped(np.random.permutation(T)[:V]),
        "n3": striped8(np.stack([np.random.permutation(V) for _ in range(8)])),
        "n4": striped8(np.stack([np.random.permutation(V) for _ in range(8)])),
        "n5": striped8(np.stack([np.random.permutation(V) for _ in range(8)])),
        "n6": striped8(np.stack([np.random.permutation(V) for _ in range(8)])),
    }


def reference(x_words, x_scales, w1_words, w1_scales, w2_words, w2_scales, w3_words, w3_scales, ga, gb, offs, two, n1, n2, three, n3, n4, n5, n6):
    xq = unpack_weight(x_words, x_scales)[:, unstriped(offs)]
    y = unpack_weight(w1_words, w1_scales).T @ xq
    x_two = unpack_weight(x_words, x_scales)[:, unstriped(two)]
    d = unpack_weight(w2_words, w2_scales).T @ x_two
    z = f64(ga) * (0.75 * (y * (d[np.arange(H)[:, None], runs(n2, H)]) - ((y[np.arange(H)[:, None], runs(n1, H)]) * d)))
    x_three = unpack_weight(x_words, x_scales)[:, unstriped(three)]
    b = unpack_weight(w3_words, w3_scales).T @ x_three
    st = b - (b[np.arange(H)[:, None], runs(n3, H)])
    z2 = f64(gb) * (st / (np.abs(st[np.arange(H)[:, None], runs(n4, H)]) + 0.5))
    s = 0.0625 * ((mxq(z, 0, "e4m3").T @ mxq(z2, 0, "e4m3")))
    st2 = np.maximum(s, s[np.arange(S)[:, None], runs(n5, S)])
    out_0 = st2[np.arange(S)[:, None], runs(n6, S)] - (0.5 * s)
    return (out_0,) + planes(out_0)

@@ -1,0 +1,244 @@
+from contextlib import ExitStack
+
+import concourse.mybir as mybir
+
+F32 = mybir.dt.float32
+BF16 = mybir.dt.bfloat16
+I32 = mybir.dt.int32
+U32 = mybir.dt.uint32
+U16 = mybir.dt.uint16
+U8 = mybir.dt.uint8
+FP8X4 = mybir.dt.float8_e4m3fn_x4
+ALU = mybir.AluOpType
+ACT = mybir.ActivationFunctionType
+
+P = 128
+PACK = 4
+T = 2048
+S = 512
+HALF = S // 2
+BIG = 2.0 ** 127
+FLOPS = 4 * 2 * 512 * 512 * 512
+
+
+def tile_picked_twkcrossbhopnhopb_none_po_kernel(
+    tc, x_words, x_scales, w1_words, w1_scales, w2_words, w2_scales, w3_words, w3_scales,
+    ga, gb, offs, two, n1, n2, three, n3, n4, n5, n6, out_0, out_1, out_2,
+):
+    nc = tc.nc
+    with ExitStack() as ctx:
+        lists = ctx.enter_context(tc.tile_pool(name="lists", bufs=1))
+        keep = ctx.enter_context(tc.tile_pool(name="keep", bufs=1))
+        psum = ctx.enter_context(tc.psum_pool(name="psum", bufs=8))
+
+        def load_list(ap, name):
+            tile = lists.tile([P, S // 16], U16, name=name)
+            nc.sync.dma_start(tile[:], ap)
+            return tile
+
+        def load_words(ap, width, name):
+            tile = keep.tile([P, width], U32, name=name, align_bytes=64)
+            nc.sync.dma_start(tile[:].bitcast(I32), ap[0].rearrange("p n r -> p (n r)").bitcast(I32))
+            return tile
+
+        def load_scales(tile, ap, row):
+            for q in range(4):
+                nc.sync.dma_start(
+                    tile[32 * q + row : 32 * q + row + 4, :].bitcast(I32), ap[0, 4 * q : 4 * q + 4, :].bitcast(I32)
+                )
+
+        def zeroed_bytes(width, name):
+            tile = keep.tile([P, width], U8, name=name, align_bytes=64)
+            nc.vector.memset(tile[:].bitcast(I32), 0)
+            return tile
+
+        def gather(window, offsets, dtype, name):
+            tile = keep.tile([P, S], dtype, name=name, align_bytes=64)
+            nc.vector.tensor_copy(tile[:], window[:].indirect(offsets[:]))
+            return tile
+
+        def deal(raw, dtype, run, name):
+            tile = keep.tile([P, S], dtype, name=name, align_bytes=64)
+            nc.vector.tensor_copy(
+                tile[:].rearrange("p (t c i) -> p c t i", t=PACK, i=run),
+                raw[:].rearrange("p (c i t) -> p c t i", t=PACK, i=run),
+            )
+            return tile
+
+        def product(lhs_words, lhs_scales, rhs_words, rhs_scales):
+            acc = psum.tile([P, S], F32, name="acc")
+            nc.tensor.matmul_mx(
+                acc[:], lhsT=lhs_words.bitcast(FP8X4), lhsT_scale=lhs_scales,
+                rhs=rhs_words.bitcast(FP8X4), rhs_scale=rhs_scales, start=True, stop=True,
+            )
+            return acc
+
+        def windows(name):
+            return [keep.tile([P, 2 * S], F32, name="%s%d" % (name, t), align_bytes=64) for t in range(PACK)]
+
+        def cols(t):
+            return slice(P * t, P * (t + 1))
+
+        xs_raw = zeroed_bytes(T, "xs_raw")
+        w3s_raw = zeroed_bytes(S, "w3s_raw")
+        w12s_raw = zeroed_bytes(S, "w12s_raw")
+        b_win = windows("b_win")
+        half = keep.tile([P, 1], F32, name="half", tag="recip", align_bytes=64)
+        nc.vector.memset(half[:], 0.5)
+        for t in range(PACK):
+            nc.scalar.activation(b_win[t][:, S:], half[:].to_broadcast([P, S]), ACT.Ln)
+
+        w3_raw = load_words(w3_words, S, "w3_raw")
+        load_scales(xs_raw, x_scales, 0)
+        three_l = load_list(three, "three_l")
+        offs_l = load_list(offs, "offs_l")
+        xw_raw = load_words(x_words, T, "xw_raw")
+        load_scales(w3s_raw, w3_scales, 0)
+        gb_t = keep.tile([P, PACK], F32, name="gb_t")
+        nc.sync.dma_start(gb_t[:], gb.rearrange("(p t) o -> p (t o)", t=PACK))
+        two_l = load_list(two, "two_l")
+        n3_l = load_list(n3, "n3_l")
+        w1_raw = load_words(w1_words, S, "w1_raw")
+        w2_raw = load_words(w2_words, S, "w2_raw")
+        load_scales(w12s_raw, w1_scales, 0)
+        load_scales(w12s_raw, w2_scales, 4)
+        ga_t = keep.tile([P, PACK], F32, name="ga_t")
+        nc.sync.dma_start(ga_t[:], ga.rearrange("(p t) o -> p (t o)", t=PACK))
+        n2_l = load_list(n2, "n2_l")
+        n1_l = load_list(n1, "n1_l")
+        n4_l = load_list(n4, "n4_l")
+        n5_l = load_list(n5, "n5_l")
+        n6_l = load_list(n6, "n6_l")
+
+        three_s = gather(xs_raw, three_l, U8, "three_s")
+        offs_s = gather(xs_raw, offs_l, U8, "offs_s")
+        w3_w = deal(w3_raw, U32, 4, "w3_w")
+        three_w = gather(xw_raw, three_l, U32, "three_w")
+        w3_s = deal(w3s_raw, U8, 16, "w3_s")
+        b_acc = [product(w3_w[:, cols(t)], w3_s[:, cols(t)], three_w[:], three_s[:]) for t in range(PACK)]
+        y_win = windows("y_win")
+        d_win = windows("d_win")
+        for t in range(PACK):
+            nc.scalar.activation(b_win[t][:, :S], b_acc[t][:], ACT.Copy, scale=gb_t[:, t : t + 1])
+            nc.scalar.activation(y_win[t][:, S:], b_acc[t][:], ACT.Copy, scale=gb_t[:, t : t + 1])
+        gb_rec = keep.tile([P, PACK], F32, name="gb_rec")
+        gb_inv = keep.tile([P, PACK], F32, name="gb_inv")
+        nc.vector.reciprocal(gb_rec[:], gb_t[:])
+        nc.vector.tensor_scalar(gb_inv[:], gb_rec[:], BIG, -BIG, ALU.min, ALU.max)
+
+        two_s = gather(xs_raw, two_l, U8, "two_s")
+        offs_w = gather(xw_raw, offs_l, U32, "offs_w")
+
+        l_win = b_win
+        gst = keep.tile([P, PACK, S], F32, name="gst", align_bytes=64)
+
+        two_w = gather(xw_raw, two_l, U32, "two_w")
+        w1_w = deal(w1_raw, U32, 4, "w1_w")
+        w2_w = deal(w2_raw, U32, 4, "w2_w")
+        w12_s = deal(w12s_raw, U8, 16, "w12_s")
+        for t in range(PACK):
+            nc.vector.tensor_tensor(gst[:, t, :], b_win[t][:].indirect(n3_l[:]), y_win[t][:, S:], ALU.subtract)
+
+        left = keep.tile([P, PACK, S], F32, name="left", align_bytes=64)
+        right = keep.tile([P, PACK, S], F32, name="right", align_bytes=64)
+
+        def project(t):
+            y_acc = product(w1_w[:, cols(t)], w12_s[:, cols(t)], offs_w[:], offs_s[:])
+            d_acc = product(w2_w[:, cols(t)], w12_s[4:P, cols(t)], two_w[:], two_s[:])
+            nc.scalar.activation(y_win[t][:, :S], y_acc[:], ACT.Copy, scale=ga_t[:, t : t + 1])
+            nc.scalar.activation(d_win[t][:, :S], d_acc[:], ACT.Copy, scale=0.75)
+
+        def log_size(t):
+            nc.scalar.activation(d_win[t][:, S:], gst[:, t, :], ACT.Abs, scale=gb_inv[:, t : t + 1])
+            nc.scalar.activation(l_win[t][:, :S], d_win[t][:, S:], ACT.Ln, bias=half[:])
+
+        for t in range(PACK):
+            project(t)
+            log_size(t)
+        for t in range(PACK):
+            nc.vector.tensor_tensor(left[:, t, :], d_win[t][:].indirect(n2_l[:]), y_win[t][:, :S], ALU.mult)
+            nc.vector.tensor_tensor(right[:, t, :], y_win[t][:].indirect(n1_l[:]), d_win[t][:, :S], ALU.mult)
+
+        recip = keep.tile([P, PACK, S], F32, name="recip", tag="recip", align_bytes=64)
+        for t in range(PACK):
+            nc.scalar.activation(recip[:, t, :], l_win[t][:].indirect(n4_l[:]), ACT.Exp, scale=-1.0)
+
+        z2_b = keep.tile([P, S, PACK], BF16, name="z2_b", align_bytes=64)
+        nc.vector.tensor_tensor(
+            z2_b[:].rearrange("p (c i) k -> p c k i", i=4),
+            gst[:].rearrange("p k (c i) -> p c k i", i=4),
+            recip[:].rearrange("p k (c i) -> p c k i", i=4),
+            ALU.mult,
+        )
+        z2_w = keep.tile([P, S], U32, name="z2_w", align_bytes=64)
+        z2_s = keep.tile([P, S], U8, name="z2_s", align_bytes=64)
+        z_b = [keep.tile([P, 2, P, PACK], BF16, name="z_b%d" % u, align_bytes=64) for u in range(2)]
+        z_w = [keep.tile([P, 2 * P], U32, name="z_w%d" % u, align_bytes=64) for u in range(2)]
+        z_s = [keep.tile([P, 2 * P], U8, name="z_s%d" % u, align_bytes=64) for u in range(2)]
+
+        def round_z(u):
+            nc.vector.tensor_tensor(
+                z_b[u][:].rearrange("p t m k -> p m k t"),
+                left[:].rearrange("p k (m t) -> p m k t", t=PACK)[:, :, :, 2 * u : 2 * u + 2],
+                right[:].rearrange("p k (m t) -> p m k t", t=PACK)[:, :, :, 2 * u : 2 * u + 2],
+                ALU.subtract,
+            )
+
+        def quantise_z(u):
+            nc.vector.quantize_mx(z_w[u][:].bitcast(FP8X4), z_s[u][:], z_b[u][:].rearrange("p t m k -> p (t m k)"))
+
+        round_z(0)
+        nc.vector.quantize_mx(z2_w[:].bitcast(FP8X4), z2_s[:], z2_b[:].rearrange("p v k -> p (v k)"))
+        quantise_z(0)
+        round_z(1)
+        quantise_z(1)
+
+        s_win = b_win
+        top_win = windows("top_win")
+        half_s = keep.tile([P, PACK, S], F32, name="half_s", align_bytes=64)
+        s_acc = []
+        for t in range(PACK):
+            s_acc.append(product(z_w[t // 2][:, cols(t % 2)], z_s[t // 2][:, cols(t % 2)], z2_w[:], z2_s[:]))
+            nc.scalar.activation(s_win[t][:, :S], s_acc[t][:], ACT.Copy, scale=-0.0625)
+        for t in range(PACK):
+            nc.scalar.activation(half_s[:, t, :], s_acc[t][:], ACT.Copy, scale=-0.03125)
+        for t in range(PACK):
+            nc.vector.tensor_copy(top_win[t][:, S:], s_win[t][:].indirect(n5_l[:]))
+            if t > 0:
+                nc.vector.tensor_tensor(top_win[t - 1][:, :S], top_win[t - 1][:, S:], s_win[t - 1][:, :S], ALU.max)
+        nc.vector.tensor_tensor(top_win[3][:, :S], top_win[3][:, S:], s_win[3][:, :S], ALU.max)
+
+        out_rows = out_0.rearrange("(p t) v -> p t v", t=PACK)
+        out_words = out_1[0].rearrange("p n r -> p (n r)").bitcast(I32)
+        o_s = keep.tile([P, S], U8, name="o_s", align_bytes=64)
+        o_f = [keep.tile([P, PACK, HALF], F32, name="o_f%d" % h, align_bytes=64) for h in range(2)]
+        o_b = [keep.tile([P, HALF, PACK], BF16, name="o_b%d" % h, align_bytes=64) for h in range(2)]
+        o_w = [keep.tile([P, HALF], U32, name="o_w%d" % h, align_bytes=64) for h in range(2)]
+
+        def result(h, t):
+            span = slice(HALF * h, HALF * (h + 1))
+            nc.vector.tensor_tensor(
+                o_f[h][:, t, :], top_win[t][:].indirect(n6_l[:, 16 * h : 16 * (h + 1)]), half_s[:, t, span], ALU.subtract
+            )
+            nc.sync.dma_start(out_rows[:, t, span], o_f[h][:, t, :])
+
+        def views(h):
+            return o_b[h][:].rearrange("p (c i) k -> p c k i", i=4), o_f[h][:].rearrange("p k (c i) -> p c k i", i=4)
+
+        def planes(h):
+            span = slice(HALF * h, HALF * (h + 1))
+            nc.vector.quantize_mx(o_w[h][:].bitcast(FP8X4), o_s[:, span], o_b[h][:].rearrange("p v k -> p (v k)"))
+            nc.scalar.dma_start(out_words[:, span], o_w[h][:].bitcast(I32))
+
+        for t in range(PACK):
+            result(0, t)
+        nc.scalar.copy(*views(0))
+        for t in range(PACK):
+            result(1, t)
+            if t == 2:
+                planes(0)
+        nc.vector.tensor_copy(*views(1))
+        planes(1)
+        for q in range(4):
+            queue = nc.sync if q % 2 == 0 else nc.scalar
+            queue.dma_start(out_2[0, 4 * q : 4 * q + 4, :].bitcast(I32), o_s[32 * q : 32 * q + 4, :].bitcast(I32))

@@ -49,7 +49,7 @@ def tile_picked_twkcrossbhopnhopb_none_po_kernel(
 
         def zeroed_bytes(width, name):
             tile = keep.tile([P, width], U8, name=name, align_bytes=64)
-            nc.vector.memset(tile[:].bitcast(I32), 0)
+            nc.gpsimd.memset(tile[:].bitcast(I32), 0)
             return tile
 
         def gather(window, offsets, dtype, name):
@@ -88,9 +88,9 @@ def tile_picked_twkcrossbhopnhopb_none_po_kernel(
         for t in range(PACK):
             nc.scalar.activation(b_win[t][:, S:], half[:].to_broadcast([P, S]), ACT.Ln)
 
-        w3_raw = load_words(w3_words, S, "w3_raw")
-        load_scales(xs_raw, x_scales, 0)
         three_l = load_list(three, "three_l")
+        load_scales(xs_raw, x_scales, 0)
+        w3_raw = load_words(w3_words, S, "w3_raw")
         offs_l = load_list(offs, "offs_l")
         xw_raw = load_words(x_words, T, "xw_raw")
         load_scales(w3s_raw, w3_scales, 0)
@@ -111,8 +111,8 @@ def tile_picked_twkcrossbhopnhopb_none_po_kernel(
         n6_l = load_list(n6, "n6_l")
 
         three_s = gather(xs_raw, three_l, U8, "three_s")
-        offs_s = gather(xs_raw, offs_l, U8, "offs_s")
         w3_w = deal(w3_raw, U32, 4, "w3_w")
+        offs_s = gather(xs_raw, offs_l, U8, "offs_s")
         three_w = gather(xw_raw, three_l, U32, "three_w")
         w3_s = deal(w3s_raw, U8, 16, "w3_s")
         b_acc = [product(w3_w[:, cols(t)], w3_s[:, cols(t)], three_w[:], three_s[:]) for t in range(PACK)]
@@ -159,17 +159,20 @@ def tile_picked_twkcrossbhopnhopb_none_po_kernel(
             nc.vector.tensor_tensor(left[:, t, :], d_win[t][:].indirect(n2_l[:]), y_win[t][:, :S], ALU.mult)
             nc.vector.tensor_tensor(right[:, t, :], y_win[t][:].indirect(n1_l[:]), d_win[t][:, :S], ALU.mult)
 
-        recip = keep.tile([P, PACK, S], F32, name="recip", tag="recip", align_bytes=64)
-        for t in range(PACK):
-            nc.scalar.activation(recip[:, t, :], l_win[t][:].indirect(n4_l[:]), ACT.Exp, scale=-1.0)
-
+        recip = keep.tile([P, 2, PACK, HALF], F32, name="recip", tag="recip", align_bytes=64)
         z2_b = keep.tile([P, S, PACK], BF16, name="z2_b", align_bytes=64)
-        nc.vector.tensor_tensor(
-            z2_b[:].rearrange("p (c i) k -> p c k i", i=4),
-            gst[:].rearrange("p k (c i) -> p c k i", i=4),
-            recip[:].rearrange("p k (c i) -> p c k i", i=4),
-            ALU.mult,
-        )
+        for h in range(2):
+            span = slice(HALF * h, HALF * (h + 1))
+            for t in range(PACK):
+                nc.scalar.activation(
+                    recip[:, h, t, :], l_win[t][:].indirect(n4_l[:, 16 * h : 16 * (h + 1)]), ACT.Exp, scale=-1.0
+                )
+            nc.vector.tensor_tensor(
+                z2_b[:, span, :].rearrange("p (c i) k -> p c k i", i=4),
+                gst[:, :, span].rearrange("p k (c i) -> p c k i", i=4),
+                recip[:, h, :, :].rearrange("p k (c i) -> p c k i", i=4),
+                ALU.mult,
+            )
         z2_w = keep.tile([P, S], U32, name="z2_w", align_bytes=64)
         z2_s = keep.tile([P, S], U8, name="z2_s", align_bytes=64)
         z_b = [keep.tile([P, 2, P, PACK], BF16, name="z_b%d" % u, align_bytes=64) for u in range(2)]
@@ -188,8 +191,8 @@ def tile_picked_twkcrossbhopnhopb_none_po_kernel(
             nc.vector.quantize_mx(z_w[u][:].bitcast(FP8X4), z_s[u][:], z_b[u][:].rearrange("p t m k -> p (t m k)"))
 
         round_z(0)
-        nc.vector.quantize_mx(z2_w[:].bitcast(FP8X4), z2_s[:], z2_b[:].rearrange("p v k -> p (v k)"))
         quantise_z(0)
+        nc.vector.quantize_mx(z2_w[:].bitcast(FP8X4), z2_s[:], z2_b[:].rearrange("p v k -> p (v k)"))
         round_z(1)
         quantise_z(1)
 
@@ -220,25 +223,38 @@ def tile_picked_twkcrossbhopnhopb_none_po_kernel(
             nc.vector.tensor_tensor(
                 o_f[h][:, t, :], top_win[t][:].indirect(n6_l[:, 16 * h : 16 * (h + 1)]), half_s[:, t, span], ALU.subtract
             )
-            nc.sync.dma_start(out_rows[:, t, span], o_f[h][:, t, :])
+            if t % 2 == 1:
+                nc.sync.dma_start(out_rows[:, t - 1 : t + 1, span], o_f[h][:, t - 1 : t + 1, :])
 
-        def views(h):
-            return o_b[h][:].rearrange("p (c i) k -> p c k i", i=4), o_f[h][:].rearrange("p k (c i) -> p c k i", i=4)
+        def views(h, span):
+            return (
+                o_b[h][:, span, :].rearrange("p (c i) k -> p c k i", i=4),
+                o_f[h][:, :, span].rearrange("p k (c i) -> p c k i", i=4),
+            )
 
-        def planes(h):
-            span = slice(HALF * h, HALF * (h + 1))
-            nc.vector.quantize_mx(o_w[h][:].bitcast(FP8X4), o_s[:, span], o_b[h][:].rearrange("p v k -> p (v k)"))
-            nc.scalar.dma_start(out_words[:, span], o_w[h][:].bitcast(I32))
+        def quantise_out(h, first, width):
+            nc.vector.quantize_mx(
+                o_w[h][:, first : first + width].bitcast(FP8X4),
+                o_s[:, HALF * h + first : HALF * h + first + width],
+                o_b[h][:, first : first + width, :].rearrange("p v k -> p (v k)"),
+            )
+
+        def store_words(h):
+            nc.scalar.dma_start(out_words[:, HALF * h : HALF * (h + 1)], o_w[h][:].bitcast(I32))
 
         for t in range(PACK):
             result(0, t)
-        nc.scalar.copy(*views(0))
+        nc.scalar.copy(*views(0, slice(0, HALF)))
         for t in range(PACK):
             result(1, t)
             if t == 2:
-                planes(0)
-        nc.vector.tensor_copy(*views(1))
-        planes(1)
+                quantise_out(0, 0, HALF)
+                store_words(0)
+        nc.scalar.copy(*views(1, slice(P, HALF)))
+        nc.vector.tensor_copy(*views(1, slice(0, P)))
+        quantise_out(1, 0, P)
+        quantise_out(1, P, P)
+        store_words(1)
         for q in range(4):
             queue = nc.sync if q % 2 == 0 else nc.scalar
             queue.dma_start(out_2[0, 4 * q : 4 * q + 4, :].bitcast(I32), o_s[32 * q : 32 * q + 4, :].bitcast(I32))

@@ -41,19 +41,19 @@ def tile_picked_twkcrossbhopnhopb_none_po_kernel(
             nc.sync.dma_start(tile[:].bitcast(I32), ap[0].rearrange("p n r -> p (n r)").bitcast(I32))
             return tile
 
-        def load_scales(tile, ap, row):
+        def load_scales(tile, ap, row, queue=nc.sync):
             for q in range(4):
-                nc.sync.dma_start(
+                queue.dma_start(
                     tile[32 * q + row : 32 * q + row + 4, :].bitcast(I32), ap[0, 4 * q : 4 * q + 4, :].bitcast(I32)
                 )
 
         def zeroed_bytes(width, name):
-            tile = keep.tile([P, width], U8, name=name, align_bytes=64)
+            tile = keep.tile([P, width], U8, name=name, tag=name, align_bytes=64)
             nc.gpsimd.memset(tile[:].bitcast(I32), 0)
             return tile
 
-        def gather(window, offsets, dtype, name):
-            tile = keep.tile([P, S], dtype, name=name, align_bytes=64)
+        def gather(window, offsets, dtype, name, tag=None):
+            tile = keep.tile([P, S], dtype, name=name, tag=tag or name, align_bytes=64)
             nc.vector.tensor_copy(tile[:], window[:].indirect(offsets[:]))
             return tile
 
@@ -83,10 +83,11 @@ def tile_picked_twkcrossbhopnhopb_none_po_kernel(
         w3s_raw = zeroed_bytes(S, "w3s_raw")
         w12s_raw = zeroed_bytes(S, "w12s_raw")
         b_win = windows("b_win")
+        d_win = windows("d_win")
         half = keep.tile([P, 1], F32, name="half", tag="recip", align_bytes=64)
         nc.vector.memset(half[:], 0.5)
-        for t in range(PACK):
-            nc.scalar.activation(b_win[t][:, S:], half[:].to_broadcast([P, S]), ACT.Ln)
+        for win in b_win + d_win:
+            nc.scalar.activation(win[:, S:], half[:].to_broadcast([P, S]), ACT.Ln)
 
         three_l = load_list(three, "three_l")
         load_scales(xs_raw, x_scales, 0)
@@ -101,9 +102,12 @@ def tile_picked_twkcrossbhopnhopb_none_po_kernel(
         w1_raw = load_words(w1_words, S, "w1_raw")
         w2_raw = load_words(w2_words, S, "w2_raw")
         load_scales(w12s_raw, w1_scales, 0)
-        load_scales(w12s_raw, w2_scales, 4)
-        ga_t = keep.tile([P, PACK], F32, name="ga_t")
-        nc.sync.dma_start(ga_t[:], ga.rearrange("(p t) o -> p (t o)", t=PACK))
+        load_scales(w12s_raw, w2_scales, 4, nc.gpsimd)
+        size = keep.tile([P, PACK, S], F32, name="size", align_bytes=64)
+        ga_t = size[:, 0, 0:PACK]
+        d_scale = size[:, 1, 0:1]
+        nc.vector.memset(d_scale, 0.75)
+        nc.sync.dma_start(ga_t, ga.rearrange("(p t) o -> p (t o)", t=PACK))
         n2_l = load_list(n2, "n2_l")
         n1_l = load_list(n1, "n1_l")
         n4_l = load_list(n4, "n4_l")
@@ -117,7 +121,6 @@ def tile_picked_twkcrossbhopnhopb_none_po_kernel(
         w3_s = deal(w3s_raw, U8, 16, "w3_s")
         b_acc = [product(w3_w[:, cols(t)], w3_s[:, cols(t)], three_w[:], three_s[:]) for t in range(PACK)]
         y_win = windows("y_win")
-        d_win = windows("d_win")
         for t in range(PACK):
             nc.scalar.activation(b_win[t][:, :S], b_acc[t][:], ACT.Copy, scale=gb_t[:, t : t + 1])
             nc.scalar.activation(y_win[t][:, S:], b_acc[t][:], ACT.Copy, scale=gb_t[:, t : t + 1])
@@ -127,15 +130,15 @@ def tile_picked_twkcrossbhopnhopb_none_po_kernel(
         nc.vector.tensor_scalar(gb_inv[:], gb_rec[:], BIG, -BIG, ALU.min, ALU.max)
 
         two_s = gather(xs_raw, two_l, U8, "two_s")
-        offs_w = gather(xw_raw, offs_l, U32, "offs_w")
+        offs_w = gather(xw_raw, offs_l, U32, "offs_w", "w3s_raw")
 
         l_win = b_win
-        gst = keep.tile([P, PACK, S], F32, name="gst", align_bytes=64)
 
         two_w = gather(xw_raw, two_l, U32, "two_w")
         w1_w = deal(w1_raw, U32, 4, "w1_w")
         w2_w = deal(w2_raw, U32, 4, "w2_w")
         w12_s = deal(w12s_raw, U8, 16, "w12_s")
+        gst = keep.tile([P, PACK, S], F32, name="gst", tag="w12s_raw", align_bytes=64)
         for t in range(PACK):
             nc.vector.tensor_tensor(gst[:, t, :], b_win[t][:].indirect(n3_l[:]), y_win[t][:, S:], ALU.subtract)
 
@@ -146,21 +149,27 @@ def tile_picked_twkcrossbhopnhopb_none_po_kernel(
             y_acc = product(w1_w[:, cols(t)], w12_s[:, cols(t)], offs_w[:], offs_s[:])
             d_acc = product(w2_w[:, cols(t)], w12_s[4:P, cols(t)], two_w[:], two_s[:])
             nc.scalar.activation(y_win[t][:, :S], y_acc[:], ACT.Copy, scale=ga_t[:, t : t + 1])
-            nc.scalar.activation(d_win[t][:, :S], d_acc[:], ACT.Copy, scale=0.75)
+            nc.scalar.activation(d_win[t][:, :S], d_acc[:], ACT.Copy, scale=d_scale)
 
         def log_size(t):
-            nc.scalar.activation(d_win[t][:, S:], gst[:, t, :], ACT.Abs, scale=gb_inv[:, t : t + 1])
-            nc.scalar.activation(l_win[t][:, :S], d_win[t][:, S:], ACT.Ln, bias=half[:])
+            nc.scalar.activation(size[:, t, :], gst[:, t, :], ACT.Abs, scale=gb_inv[:, t : t + 1])
+
+        def log(t):
+            nc.scalar.activation(l_win[t][:, :S], size[:, t, :], ACT.Ln, bias=half[:])
 
         for t in range(PACK):
             project(t)
+        log_size(0)
+        for t in range(1, PACK):
             log_size(t)
+            log(t - 1)
+        log(PACK - 1)
         for t in range(PACK):
             nc.vector.tensor_tensor(left[:, t, :], d_win[t][:].indirect(n2_l[:]), y_win[t][:, :S], ALU.mult)
             nc.vector.tensor_tensor(right[:, t, :], y_win[t][:].indirect(n1_l[:]), d_win[t][:, :S], ALU.mult)
 
         recip = keep.tile([P, 2, PACK, HALF], F32, name="recip", tag="recip", align_bytes=64)
-        z2_b = keep.tile([P, S, PACK], BF16, name="z2_b", align_bytes=64)
+        z2_b = keep.tile([P, S, PACK], BF16, name="z2_b", tag="rounded", align_bytes=64)
         for h in range(2):
             span = slice(HALF * h, HALF * (h + 1))
             for t in range(PACK):
@@ -175,26 +184,30 @@ def tile_picked_twkcrossbhopnhopb_none_po_kernel(
             )
         z2_w = keep.tile([P, S], U32, name="z2_w", align_bytes=64)
         z2_s = keep.tile([P, S], U8, name="z2_s", align_bytes=64)
-        z_b = [keep.tile([P, 2, P, PACK], BF16, name="z_b%d" % u, align_bytes=64) for u in range(2)]
-        z_w = [keep.tile([P, 2 * P], U32, name="z_w%d" % u, align_bytes=64) for u in range(2)]
         z_s = [keep.tile([P, 2 * P], U8, name="z_s%d" % u, align_bytes=64) for u in range(2)]
 
-        def round_z(u):
+        def round_z(u, z_b):
             nc.vector.tensor_tensor(
-                z_b[u][:].rearrange("p t m k -> p m k t"),
+                z_b.rearrange("p t m k -> p m k t"),
                 left[:].rearrange("p k (m t) -> p m k t", t=PACK)[:, :, :, 2 * u : 2 * u + 2],
                 right[:].rearrange("p k (m t) -> p m k t", t=PACK)[:, :, :, 2 * u : 2 * u + 2],
                 ALU.subtract,
             )
 
-        def quantise_z(u):
-            nc.vector.quantize_mx(z_w[u][:].bitcast(FP8X4), z_s[u][:], z_b[u][:].rearrange("p t m k -> p (t m k)"))
+        def quantise_z(u, z_b, words):
+            nc.vector.quantize_mx(words[:].bitcast(FP8X4), z_s[u][:], z_b.rearrange("p t m k -> p (t m k)"))
 
-        round_z(0)
-        quantise_z(0)
+        z_b0_tile = keep.tile([P, 2, P, PACK], BF16, name="z_b0", align_bytes=64)
+        z_b0 = z_b0_tile[:]
+        round_z(0, z_b0)
+        z_w0 = keep.tile([P, 2 * P], U32, name="z_w0", align_bytes=64)
+        quantise_z(0, z_b0, z_w0)
         nc.vector.quantize_mx(z2_w[:].bitcast(FP8X4), z2_s[:], z2_b[:].rearrange("p v k -> p (v k)"))
-        round_z(1)
-        quantise_z(1)
+        z_b1 = z2_b[:, :HALF, :].rearrange("p (t m) k -> p t m k", t=2)
+        round_z(1, z_b1)
+        z_w1 = keep.tile([P, 2 * P], U32, name="z_w1", align_bytes=64)
+        quantise_z(1, z_b1, z_w1)
+        z_w = [z_w0, z_w1]
 
         s_win = b_win
         top_win = windows("top_win")

from contextlib import ExitStack

import concourse.mybir as mybir

F32 = mybir.dt.float32
BF16 = mybir.dt.bfloat16
I32 = mybir.dt.int32
U32 = mybir.dt.uint32
U16 = mybir.dt.uint16
U8 = mybir.dt.uint8
FP8X4 = mybir.dt.float8_e4m3fn_x4
ALU = mybir.AluOpType
ACT = mybir.ActivationFunctionType

P = 128
PACK = 4
T = 2048
S = 512
HALF = S // 2
BIG = 2.0 ** 127
FLOPS = 4 * 2 * 512 * 512 * 512


def tile_picked_twkcrossbhopnhopb_none_po_kernel(
    tc, x_words, x_scales, w1_words, w1_scales, w2_words, w2_scales, w3_words, w3_scales,
    ga, gb, offs, two, n1, n2, three, n3, n4, n5, n6, out_0, out_1, out_2,
):
    nc = tc.nc
    with ExitStack() as ctx:
        lists = ctx.enter_context(tc.tile_pool(name="lists", bufs=1))
        keep = ctx.enter_context(tc.tile_pool(name="keep", bufs=1))
        psum = ctx.enter_context(tc.psum_pool(name="psum", bufs=8))

        def load_list(ap, name):
            tile = lists.tile([P, S // 16], U16, name=name)
            nc.sync.dma_start(tile[:], ap)
            return tile

        def load_words(ap, width, name):
            tile = keep.tile([P, width], U32, name=name, align_bytes=64)
            nc.sync.dma_start(tile[:].bitcast(I32), ap[0].rearrange("p n r -> p (n r)").bitcast(I32))
            return tile

        def load_scales(tile, ap, row, queue=nc.sync):
            for q in range(4):
                queue.dma_start(
                    tile[32 * q + row : 32 * q + row + 4, :].bitcast(I32), ap[0, 4 * q : 4 * q + 4, :].bitcast(I32)
                )

        def zeroed_bytes(width, name):
            tile = keep.tile([P, width], U8, name=name, tag=name, align_bytes=64)
            nc.gpsimd.memset(tile[:].bitcast(I32), 0)
            return tile

        def gather(window, offsets, dtype, name, tag=None):
            tile = keep.tile([P, S], dtype, name=name, tag=tag or name, align_bytes=64)
            nc.vector.tensor_copy(tile[:], window[:].indirect(offsets[:]))
            return tile

        def deal(raw, dtype, run, name):
            tile = keep.tile([P, S], dtype, name=name, align_bytes=64)
            nc.vector.tensor_copy(
                tile[:].rearrange("p (t c i) -> p c t i", t=PACK, i=run),
                raw[:].rearrange("p (c i t) -> p c t i", t=PACK, i=run),
            )
            return tile

        def product(lhs_words, lhs_scales, rhs_words, rhs_scales):
            acc = psum.tile([P, S], F32, name="acc")
            nc.tensor.matmul_mx(
                acc[:], lhsT=lhs_words.bitcast(FP8X4), lhsT_scale=lhs_scales,
                rhs=rhs_words.bitcast(FP8X4), rhs_scale=rhs_scales, start=True, stop=True,
            )
            return acc

        def windows(name):
            return [keep.tile([P, 2 * S], F32, name="%s%d" % (name, t), align_bytes=64) for t in range(PACK)]

        def cols(t):
            return slice(P * t, P * (t + 1))

        xs_raw = zeroed_bytes(T, "xs_raw")
        w3s_raw = zeroed_bytes(S, "w3s_raw")
        w12s_raw = zeroed_bytes(S, "w12s_raw")
        b_win = windows("b_win")
        d_win = windows("d_win")
        half = keep.tile([P, 1], F32, name="half", tag="recip", align_bytes=64)
        nc.vector.memset(half[:], 0.5)
        for win in b_win + d_win:
            nc.scalar.activation(win[:, S:], half[:].to_broadcast([P, S]), ACT.Ln)

        three_l = load_list(three, "three_l")
        load_scales(xs_raw, x_scales, 0)
        w3_raw = load_words(w3_words, S, "w3_raw")
        offs_l = load_list(offs, "offs_l")
        xw_raw = load_words(x_words, T, "xw_raw")
        load_scales(w3s_raw, w3_scales, 0)
        gb_t = keep.tile([P, PACK], F32, name="gb_t")
        nc.sync.dma_start(gb_t[:], gb.rearrange("(p t) o -> p (t o)", t=PACK))
        two_l = load_list(two, "two_l")
        n3_l = load_list(n3, "n3_l")
        w1_raw = load_words(w1_words, S, "w1_raw")
        w2_raw = load_words(w2_words, S, "w2_raw")
        load_scales(w12s_raw, w1_scales, 0)
        load_scales(w12s_raw, w2_scales, 4, nc.gpsimd)
        size = keep.tile([P, PACK, S], F32, name="size", align_bytes=64)
        ga_t = size[:, 0, 0:PACK]
        d_scale = size[:, 1, 0:1]
        nc.vector.memset(d_scale, 0.75)
        nc.sync.dma_start(ga_t, ga.rearrange("(p t) o -> p (t o)", t=PACK))
        n2_l = load_list(n2, "n2_l")
        n1_l = load_list(n1, "n1_l")
        n4_l = load_list(n4, "n4_l")
        n5_l = load_list(n5, "n5_l")
        n6_l = load_list(n6, "n6_l")

        three_s = gather(xs_raw, three_l, U8, "three_s")
        w3_w = deal(w3_raw, U32, 4, "w3_w")
        offs_s = gather(xs_raw, offs_l, U8, "offs_s")
        three_w = gather(xw_raw, three_l, U32, "three_w")
        w3_s = deal(w3s_raw, U8, 16, "w3_s")
        b_acc = [product(w3_w[:, cols(t)], w3_s[:, cols(t)], three_w[:], three_s[:]) for t in range(PACK)]
        y_win = windows("y_win")
        for t in range(PACK):
            nc.scalar.activation(b_win[t][:, :S], b_acc[t][:], ACT.Copy, scale=gb_t[:, t : t + 1])
            nc.scalar.activation(y_win[t][:, S:], b_acc[t][:], ACT.Copy, scale=gb_t[:, t : t + 1])
        gb_rec = keep.tile([P, PACK], F32, name="gb_rec")
        gb_inv = keep.tile([P, PACK], F32, name="gb_inv")
        nc.vector.reciprocal(gb_rec[:], gb_t[:])
        nc.vector.tensor_scalar(gb_inv[:], gb_rec[:], BIG, -BIG, ALU.min, ALU.max)

        two_s = gather(xs_raw, two_l, U8, "two_s")
        offs_w = gather(xw_raw, offs_l, U32, "offs_w", "w3s_raw")

        l_win = b_win

        two_w = gather(xw_raw, two_l, U32, "two_w")
        w1_w = deal(w1_raw, U32, 4, "w1_w")
        w2_w = deal(w2_raw, U32, 4, "w2_w")
        w12_s = deal(w12s_raw, U8, 16, "w12_s")
        gst = keep.tile([P, PACK, S], F32, name="gst", tag="w12s_raw", align_bytes=64)
        for t in range(PACK):
            nc.vector.tensor_tensor(gst[:, t, :], b_win[t][:].indirect(n3_l[:]), y_win[t][:, S:], ALU.subtract)

        left = keep.tile([P, PACK, S], F32, name="left", align_bytes=64)
        right = keep.tile([P, PACK, S], F32, name="right", align_bytes=64)

        def project(t):
            y_acc = product(w1_w[:, cols(t)], w12_s[:, cols(t)], offs_w[:], offs_s[:])
            d_acc = product(w2_w[:, cols(t)], w12_s[4:P, cols(t)], two_w[:], two_s[:])
            nc.scalar.activation(y_win[t][:, :S], y_acc[:], ACT.Copy, scale=ga_t[:, t : t + 1])
            nc.scalar.activation(d_win[t][:, :S], d_acc[:], ACT.Copy, scale=d_scale)

        def log_size(t):
            nc.scalar.activation(size[:, t, :], gst[:, t, :], ACT.Abs, scale=gb_inv[:, t : t + 1])

        def log(t):
            nc.scalar.activation(l_win[t][:, :S], size[:, t, :], ACT.Ln, bias=half[:])

        for t in range(PACK):
            project(t)
        log_size(0)
        for t in range(1, PACK):
            log_size(t)
            log(t - 1)
        log(PACK - 1)
        for t in range(PACK):
            nc.vector.tensor_tensor(left[:, t, :], d_win[t][:].indirect(n2_l[:]), y_win[t][:, :S], ALU.mult)
            nc.vector.tensor_tensor(right[:, t, :], y_win[t][:].indirect(n1_l[:]), d_win[t][:, :S], ALU.mult)

        recip = keep.tile([P, 2, PACK, HALF], F32, name="recip", tag="recip", align_bytes=64)
        z2_b = keep.tile([P, S, PACK], BF16, name="z2_b", tag="rounded", align_bytes=64)
        for h in range(2):
            span = slice(HALF * h, HALF * (h + 1))
            for t in range(PACK):
                nc.scalar.activation(
                    recip[:, h, t, :], l_win[t][:].indirect(n4_l[:, 16 * h : 16 * (h + 1)]), ACT.Exp, scale=-1.0
                )
            nc.vector.tensor_tensor(
                z2_b[:, span, :].rearrange("p (c i) k -> p c k i", i=4),
                gst[:, :, span].rearrange("p k (c i) -> p c k i", i=4),
                recip[:, h, :, :].rearrange("p k (c i) -> p c k i", i=4),
                ALU.mult,
            )
        z2_w = keep.tile([P, S], U32, name="z2_w", align_bytes=64)
        z2_s = keep.tile([P, S], U8, name="z2_s", align_bytes=64)
        z_s = [keep.tile([P, 2 * P], U8, name="z_s%d" % u, align_bytes=64) for u in range(2)]

        def round_z(u, z_b):
            nc.vector.tensor_tensor(
                z_b.rearrange("p t m k -> p m k t"),
                left[:].rearrange("p k (m t) -> p m k t", t=PACK)[:, :, :, 2 * u : 2 * u + 2],
                right[:].rearrange("p k (m t) -> p m k t", t=PACK)[:, :, :, 2 * u : 2 * u + 2],
                ALU.subtract,
            )

        def quantise_z(u, z_b, words):
            nc.vector.quantize_mx(words[:].bitcast(FP8X4), z_s[u][:], z_b.rearrange("p t m k -> p (t m k)"))

        z_b0_tile = keep.tile([P, 2, P, PACK], BF16, name="z_b0", align_bytes=64)
        z_b0 = z_b0_tile[:]
        round_z(0, z_b0)
        z_w0 = keep.tile([P, 2 * P], U32, name="z_w0", align_bytes=64)
        quantise_z(0, z_b0, z_w0)
        nc.vector.quantize_mx(z2_w[:].bitcast(FP8X4), z2_s[:], z2_b[:].rearrange("p v k -> p (v k)"))
        z_b1 = z2_b[:, :HALF, :].rearrange("p (t m) k -> p t m k", t=2)
        round_z(1, z_b1)
        z_w1 = keep.tile([P, 2 * P], U32, name="z_w1", align_bytes=64)
        quantise_z(1, z_b1, z_w1)
        z_w = [z_w0, z_w1]

        s_win = b_win
        top_win = windows("top_win")
        half_s = keep.tile([P, PACK, S], F32, name="half_s", align_bytes=64)
        s_acc = []
        for t in range(PACK):
            s_acc.append(product(z_w[t // 2][:, cols(t % 2)], z_s[t // 2][:, cols(t % 2)], z2_w[:], z2_s[:]))
            nc.scalar.activation(s_win[t][:, :S], s_acc[t][:], ACT.Copy, scale=-0.0625)
        for t in range(PACK):
            nc.scalar.activation(half_s[:, t, :], s_acc[t][:], ACT.Copy, scale=-0.03125)
        for t in range(PACK):
            nc.vector.tensor_copy(top_win[t][:, S:], s_win[t][:].indirect(n5_l[:]))
            if t > 0:
                nc.vector.tensor_tensor(top_win[t - 1][:, :S], top_win[t - 1][:, S:], s_win[t - 1][:, :S], ALU.max)
        nc.vector.tensor_tensor(top_win[3][:, :S], top_win[3][:, S:], s_win[3][:, :S], ALU.max)

        out_rows = out_0.rearrange("(p t) v -> p t v", t=PACK)
        out_words = out_1[0].rearrange("p n r -> p (n r)").bitcast(I32)
        o_s = keep.tile([P, S], U8, name="o_s", align_bytes=64)
        o_f = [keep.tile([P, PACK, HALF], F32, name="o_f%d" % h, align_bytes=64) for h in range(2)]
        o_b = [keep.tile([P, HALF, PACK], BF16, name="o_b%d" % h, align_bytes=64) for h in range(2)]
        o_w = [keep.tile([P, HALF], U32, name="o_w%d" % h, align_bytes=64) for h in range(2)]

        def result(h, t):
            span = slice(HALF * h, HALF * (h + 1))
            nc.vector.tensor_tensor(
                o_f[h][:, t, :], top_win[t][:].indirect(n6_l[:, 16 * h : 16 * (h + 1)]), half_s[:, t, span], ALU.subtract
            )
            if t % 2 == 1:
                nc.sync.dma_start(out_rows[:, t - 1 : t + 1, span], o_f[h][:, t - 1 : t + 1, :])

        def views(h, span):
            return (
                o_b[h][:, span, :].rearrange("p (c i) k -> p c k i", i=4),
                o_f[h][:, :, span].rearrange("p k (c i) -> p c k i", i=4),
            )

        def quantise_out(h, first, width):
            nc.vector.quantize_mx(
                o_w[h][:, first : first + width].bitcast(FP8X4),
                o_s[:, HALF * h + first : HALF * h + first + width],
                o_b[h][:, first : first + width, :].rearrange("p v k -> p (v k)"),
            )

        def store_words(h):
            nc.scalar.dma_start(out_words[:, HALF * h : HALF * (h + 1)], o_w[h][:].bitcast(I32))

        for t in range(PACK):
            result(0, t)
        nc.scalar.copy(*views(0, slice(0, HALF)))
        for t in range(PACK):
            result(1, t)
            if t == 2:
                quantise_out(0, 0, HALF)
                store_words(0)
        nc.scalar.copy(*views(1, slice(P, HALF)))
        nc.vector.tensor_copy(*views(1, slice(0, P)))
        quantise_out(1, 0, P)
        quantise_out(1, P, P)
        store_words(1)
        for q in range(4):
            queue = nc.sync if q % 2 == 0 else nc.scalar
            queue.dma_start(out_2[0, 4 * q : 4 * q + 4, :].bitcast(I32), o_s[32 * q : 32 * q + 4, :].bitcast(I32))
